import numpy as np, ml_dtypes
CORES = [5,29,101,125,133,157,229,253]
N = 8
BF = ml_dtypes.bfloat16
B, S, D, SH = 1, 4096, 8192, 4
W, BC = N * B, 32
LAST = (2 * 255 * 255) >> SH
def middle(m):
    return 16 * (m % 16) + 8, 16 * (m // 16) + 8
def index(p, x, y):
    return ((x - int(p[0])) ** 2 + (y - int(p[1])) ** 2) >> SH
def loud(d, rng, cells):
    t = rng.integers(0, S, (N, 8)); sg = rng.choice(np.array([-15.0, 15.0]), 16); v = d["tr"].reshape(N, 8, 16, S); x, y = middle(np.array(cells))
    ld = sg - np.sign(sg) * rng.integers(0, 2, (N, 8, 16))
    for q in range(N):
        for g in range(8):
            d["tau"][q, g, index(d["pos"][q, g], x, y)] = t[q, g]; v[q, g, :, t[q, g]] = ld[q, g].astype(BF)
    return t, ld
def setup_inputs(rng):
    tr = rng.integers(-15, 16, (N, 128, S), dtype=np.int8).astype(np.float32).astype(BF)
    pos = rng.integers(0, 256, (N, 8, 2)).astype(np.int32)
    t = np.floor(np.sqrt(np.arange(D) / D) * (rng.random((N, 8, 1)) * 0.5 + 0.25) * S).astype(np.int64) + rng.integers(0, S // 4, (N, 8, D))
    return {"tr": tr, "pos": pos, "tau": t.astype(np.int32)}
def setup_inputs_ends(rng):
    d = setup_inputs(rng); c = np.array([[0, 0], [0, 255], [255, 0], [255, 255]])
    d["pos"] = np.stack([c[rng.permutation(8) % 4] for q in range(N)]).astype(np.int32)
    t = rng.integers(0, S, (N, 8, D)); t[:, :, 0] = 0; t[:, :, LAST] = S - 1; d["tau"] = t.astype(np.int32)
    e = rng.integers(0, 2, W); e[0] = 0; e[W - 1] = 1
    loud(d, rng, np.arange(W) * BC + e * (BC - 1)); return d
def setup_inputs_ties(rng):
    d = setup_inputs(rng); s = int(rng.integers(0, 3)); cells = []
    for k in range(W):
        z = (k + s) % 3; o = [0, BC - 1] if z == 0 else rng.choice(BC, 2, replace=False) if z == 1 else range(BC)
        cells += [k * BC + int(i) for i in o]
    loud(d, rng, cells); return d
def setup_inputs_close(rng):
    d = setup_inputs(rng); k = np.arange(W); lo = k * BC + rng.integers(0, BC // 2, W); hi = k * BC + BC // 2 + rng.integers(0, BC // 2, W); x, y = middle(lo)
    d["pos"][k % N, k // N, 0] = x; d["pos"][k % N, k // N, 1] = y
    t, ld = loud(d, rng, np.concatenate([lo, hi])); v = d["tr"].reshape(N, 8, 16, S); m = np.abs(np.sum(ld, axis=(0, 1)))
    for i in range(W):
        q, g = i % N, i // N; u = (int(t[q, g]) + int(rng.integers(1, S))) % S; h = ld[q, g].copy(); s = int(rng.integers(0, 16))
        if i % 2:
            z = [(m[a] - m[b], a, b) for a in range(16) for b in range(16) if m[a] > m[b] + 1 and abs(h[b]) < 15]
            if z:
                s, b = min(z)[1:]; h[b] = h[b] + np.sign(h[b])
        h[s] = h[s] - np.sign(h[s])
        d["tau"][q, g, 0] = u; v[q, g, :, u] = h.astype(BF)
    return d
def setup_inputs_steps(rng):
    d = setup_inputs(rng); d["pos"] = np.repeat(rng.integers(0, 256, (N, 1, 2)), 8, axis=1).astype(np.int32)
    d["tau"] = np.repeat(rng.integers(0, S, (N, 8, D // 64)), 64, axis=2).astype(np.int32); return d
def setup_inputs_spread(rng):
    d = setup_inputs(rng); a = rng.choice(np.array([0, 1, 4, 15], np.int8), (N, 8, 1, S))
    v = np.clip(rng.integers(-15, 16, (N, 8, 16, S), dtype=np.int8), -a, a)
    d["tr"] = v.reshape(N, 128, S).astype(np.float32).astype(BF)
    d["pos"] = np.floor(256 * rng.random((N, 8, 2)) ** 3).astype(np.int32); d["tau"] = np.floor(S * rng.random((N, 8, D)) ** 3).astype(np.int32); return d
def check_inputs(d):
    bad = []; v = np.asarray(d["tr"]).astype(np.float32)
    if not ((np.abs(v) <= 15) & (np.rint(v) == v)).all(): bad.append("samples")
    if not ((d["pos"] >= 0) & (d["pos"] <= 255)).all(): bad.append("places")
    if not ((d["tau"] >= 0) & (d["tau"] < S)).all(): bad.append("times")
    return bad
def focus(v, pos, tau, x, y):
    a = np.zeros((16, len(x)), np.int64)
    for q in range(N):
        for g in range(8): a += v[q, g][:, tau[q, g][index(pos[q, g], x, y)]]
    return a
def reference(tr, pos, tau):
    v = tr.astype(np.float32).astype(np.int32).reshape(N, 8, 16, S)
    x, y = middle(np.arange(256)); c = focus(v, pos, tau, x, y)
    e = np.sum(c * c, axis=0).reshape(W, BC)
    w = np.arange(W) * BC + np.argmax(e, axis=1)
    j = np.arange(256); x = (16 * (w % 16)[:, None] + j % 16).reshape(-1); y = (16 * (w // 16)[:, None] + j // 16).reshape(-1)
    fine = focus(v, pos, tau, x, y).reshape(16, N, B * 256).transpose(1, 0, 2)
    return {"y": np.ascontiguousarray(fine).astype(np.float32), "w": np.tile(w.reshape(1, 1, W), (N, 1, 1)).astype(np.float32)}

@@ -1,0 +1,345 @@
+from concourse.bass import DstId, RemoteDMATransfer
+from concourse.mybir import AluOpType as A, ActivationFunctionType as F
+
+SB = {
+    "float32": {"cF": [128, 40], "rowx": [128, 256], "rowb": [128, 256], "rowg": [128, 128], "rown": [128, 136], "rowm": [32, 128],
+                "rowo": [128, 32], "colp": [32, 128], "rowy": [32, 128], "zero": [32, 32], "bone": [128, 128], "dsc": [128, 256],
+                "enm": [128, 32], "uU": [32, 128], "su": [32, 128], "rr": [32, 128], "f1": [32, 128], "f2": [32, 128], "f3": [32, 128],
+                "dlt": [32, 128], "prm": [32, 8], "xy": [128, 2], "dx2": [128, 1], "dy2": [128, 16], "fx2": [128, 256],
+                "fy2": [128, 256], "pm": [128, 256], "gm": [128, 256], "sc": [128, 256], "asq": [128, 32], "rmx": [32, 32],
+                "sgn": [32, 32], "cc": [32, 1], "hb": [32, 1], "bb": [32, 1], "uq": [32, 128], "wc": [32, 1], "wrow": [1, 8],
+                "yo": [128, 32]},
+    "bfloat16": {"trS": [128, 4096], "expd": [8, 128], "zsel": [128, 136], "iden": [128, 128], "posN": [8, 2], "lU": [8, 32],
+                 "x1": [128, 256], "send1": [128, 32], "land1": [128, 256], "hop1": [128, 32], "vt": [128, 8192], "x2": [128, 2048],
+                 "sendAB": [128, 128], "sendCD": [128, 128], "hop2": [128, 64], "land2": [128, 256]},
+    "int32": {"posI": [8, 2], "tauI": [128, 512], "ip": [128, 1], "cI": [128, 4], "d2l": [128, 16], "cl": [128, 16], "d2f": [128, 256],
+              "pmi": [128, 256], "d2i": [128, 128], "t1": [128, 128], "t2": [128, 128], "js": [128, 128]},
+    "uint16": {"o1": [128, 16], "o2": [128, 16], "tauU": [128, 512], "o3": [128, 128]},
+}
+SCRATCH = {n: ("sbuf", s, d) for d, b in SB.items() for n, s in b.items()}
+SCRATCH.update({"b%d" % i: ("psum", [128, 512], "float32") for i in range(8)})
+SEMAPHORES = ["cV", "cS", "cP", "cG", "dpos", "dtau", "dtr", "dw", "dy", "a1d", "a1x", "a2d", "a2x", "r1", "r2", "loc"]
+CUT = 224
+
+
+def bits(engines):
+    return sum(1 << e for e in engines)
+
+
+def plan(T, topo, src):
+    me = T.rank_of(src)
+    cross = [q for q, c in enumerate(T.cores) if not topo.may_write(src, c)]
+    same = [q for q, c in enumerate(T.cores) if q != me and q not in cross]
+    relays = [c for c in topo.cores_of(src) if c != src and topo.die(c) == topo.die(src)
+              and all(topo.may_write(c, T.cores[q]) for q in cross)]
+    part = len(cross) // len(relays)
+    return cross, same, [(c, cross[i * part:(i + 1) * part]) for i, c in enumerate(relays)]
+
+
+def dst(topo, d, src):
+    rid, pid = topo.addr(d, src)
+    return DstId(rid=rid, pnc=pid)
+
+
+def relay_program(g, core, T, topo, rank, dests):
+    sem = T.sem
+    on = topo.engines(T.cores[rank], core)
+    eng = topo.engines(core, T.cores[dests[0]])
+    half = len(eng) // 2
+    slot = slice(32 * rank, 32 * rank + 32)
+    to = [dst(topo, T.cores[q], core) for q in dests]
+    g.wait_ge(sem.r1, len(on) // 2)
+    g.remote_dma_fused([RemoteDMATransfer(dst_ids=to, dma_engine_mask=bits(eng), remote_sem=sem.a1x, srcs=[T.hop1[:]],
+                                          dsts=[T.land1[:, slot] for _ in to])], local_sem=sem.loc)
+    g.wait_ge(sem.r2, len(on))
+    g.remote_dma_fused([RemoteDMATransfer(dst_ids=[to[i]], dma_engine_mask=bits(eng[i * half:(i + 1) * half]), remote_sem=sem.a2x,
+                                          srcs=[T.hop2[:, 32 * i:32 * i + 32]], dsts=[T.land2[:, slot]])
+                        for i in range(len(to))], local_sem=sem.loc)
+    g.wait_ge(sem.loc, 2 * len(eng))
+
+
+def rank_program(g, core, T, topo):
+    rank = T.rank_of(core)
+    if rank is None:
+        for q, c in enumerate(T.cores):
+            for r, dests in plan(T, topo, c)[2]:
+                if r == core:
+                    relay_program(g, core, T, topo, q, dests)
+        return
+    cross, same, relays = plan(T, topo, core)
+    order = cross + same + [rank]
+    sem = T.sem
+    eng = {"G": g, "V": g.vector, "S": g.scalar, "P": g.tensor, "Y": g.sync}
+    total = {}
+    known = {q: {} for q in eng}
+    wrote, read = {}, {}
+
+    def wait(q, name, val):
+        if known[q].get(name, 0) < val:
+            eng[q].wait_ge(sem[name], val)
+            known[q][name] = val
+
+    def order_after(q, reads, writes):
+        need = {}
+        hs = [wrote[k] for k in reads + writes if k in wrote]
+        for k in writes:
+            hs += read.get(k, [])
+        for name, val in hs:
+            need[name] = max(need.get(name, 0), val)
+        for name in sorted(need):
+            wait(q, name, need[name])
+
+    def done(ins, name, n, reads, writes):
+        total[name] = total.get(name, 0) + n
+        ins.then_inc(sem[name], n)
+        h = (name, total[name])
+        for k in reads:
+            read.setdefault(k, []).append(h)
+        for k in writes:
+            wrote[k] = h
+            read[k] = []
+
+    def op(q, call, reads, writes, *args, **kw):
+        order_after(q, reads, writes)
+        done(call(*args, **kw), "c" + q, 1, reads, writes)
+
+    def dma(q, name, out, in_, reads, writes):
+        order_after(q, reads, writes)
+        done(eng[q].dma_start(out, in_), name, 16, reads, writes)
+
+    def mm(key, out, parts):
+        for i, (l, r, keys) in enumerate(parts):
+            order_after("P", keys, [key] if i == 0 else [])
+            ins = g.tensor.matmul(out, l, r, i == 0, i == len(parts) - 1)
+        done(ins, "cP", 1, [k for p in parts for k in p[2]], [key])
+
+    V, S = g.vector, g.scalar
+    ts = lambda reads, writes, *a: op("V", V.tensor_scalar, reads, writes, *a)
+    tt = lambda reads, writes, *a: op("V", V.tensor_tensor, reads, writes, *a)
+    cp = lambda reads, writes, *a: op("V", V.tensor_copy, reads, writes, *a)
+    act = lambda reads, writes, *a, **k: op("S", S.activation, reads, writes, *a, **k)
+    idn = lambda reads, writes, out, in_, scale, bias: act(reads, writes, out, in_, F.Identity, bias=bias, scale=scale)
+    iota = lambda w, out, pat, base, cm: op("G", g.iota, [], [w], out, pat, base, cm, allow_small_or_imprecise_dtypes=True)
+    fc = lambda i, n=128: T.cF[0:n, i:i + 1]
+
+    dma("Y", "dpos", T.posI[:], T.pos[:], [], ["posI"])
+    dma("S", "dtau", T.tauI[:], T.tau[:], [], ["tauI"])
+    dma("Y", "dtr", T.trS[0:64, :], T.tr[0:64, :], [], ["tr0"])
+    dma("S", "dtr", T.trS[64:128, :], T.tr[64:128, :], [], ["tr1"])
+    wrote["tr0"] = wrote["tr1"]
+
+    op("G", g.iota, [], ["ip"], T.ip[:], [[0, 1]], 0, 1)
+    iota("p", fc(0), [[0, 1]], 0, 1)
+    iota("rowg", T.rowg[:], [[1, 8], [0, 16]], 0, 0)
+    iota("rowx", T.rowx[:], [[0, 16], [16, 16]], 8, 0)
+    iota("rowb", T.rowb[:], [[16, 16], [0, 16]], 8, 0)
+    iota("rown", T.rown[:], [[1, 136]], 0, 0)
+    for P in range(4):
+        iota("rowy%d" % P, T.rowy[:, 32 * P:32 * P + 32], [[2, 8], [0, 2], [1, 2]], 0, 0)
+    iota("rowm", T.rowm[:], [[0, 8], [1, 16]], 0, 0)
+    for i, k in enumerate(order):
+        iota("rowo%d" % i, T.rowo[:, i::8], [[0, 4]], k, 0)
+    for P in range(4):
+        iota("colp%d" % P, T.colp[:, 32 * P:32 * P + 32], [[0, 8], [1, 2], [0, 2]], 2 * P, 0)
+    rowy, rowo, colp = ["rowy%d" % P for P in range(4)], ["rowo%d" % i for i in range(8)], ["colp%d" % P for P in range(4)]
+
+    ts(["ip"], ["i0"], T.cI[:, 0:1], T.ip[:], 15, None, A.bitwise_and)
+    ts(["ip"], ["i1"], T.cI[:, 1:2], T.ip[:], 4, None, A.logical_shift_right)
+    ts(["ip"], ["i2"], T.cI[:, 2:3], T.ip[:], 7, None, A.bitwise_and)
+    ts(["ip"], ["i3"], T.cI[:, 3:4], T.ip[:], 3, None, A.logical_shift_right)
+    cp(["i0", "i1", "i2", "i3"], ["sgkt"], T.cF[:, 1:5], T.cI[:])
+    s_, g_, k7, t_ = fc(1), fc(2), fc(3), fc(4)
+    ts(["rowg", "p"], ["expd"], T.expd[:], T.rowg[0:8, :], fc(0, 8), None, A.is_equal)
+    idn(["sgkt"], ["c16"], fc(5), s_, 16.0, 8.0)
+    idn(["sgkt"], ["sub"], fc(6), s_, -4096.0, 15.0 * 4096)
+    idn(["sgkt"], ["s8"], fc(7), s_, 8.0, 7.0)
+    ts(["rowg", "sgkt"], ["bone"], T.bone[:], T.rowg[:], g_, None, A.is_equal)
+    op("V", V.memset, [], ["zero"], T.zero[:], 0.0)
+
+    ts(["posI"], ["posN"], T.posN[:], T.posI[:], -1, None, A.mult)
+    mm("b0", T.b0[:, 0:2], [(T.expd[:], T.posN[:], ["expd", "posN"])])
+    ts(["rowx", "c16"], ["dsc0"], T.dsc[:], T.rowx[:], fc(5), 18.0 * 4096, A.is_gt, A.mult)
+    cp(["b0"], ["xy"], T.xy[:], T.b0[:, 0:2])
+    nX, nY = T.xy[:, 0:1], T.xy[:, 1:2]
+    act(["c16", "xy"], ["dx2"], T.dx2[:], fc(5), F.Square, bias=nX)
+    act(["rowx", "xy"], ["dy2"], T.dy2[:], T.rowx[:, 0:16], F.Square, bias=nY)
+    act(["rowx", "xy"], ["fx2"], T.fx2[:], T.rowx[:], F.Square, bias=nX)
+    act(["rowb", "xy"], ["fy2"], T.fy2[:], T.rowb[:], F.Square, bias=nY)
+    ts(["dy2", "dx2"], ["d2l"], T.d2l[:], T.dy2[:], T.dx2[:], None, A.add)
+    ts(["d2l"], ["cl"], T.cl[:], T.d2l[:], 4, 511, A.logical_shift_right, A.bitwise_and)
+    cp(["cl"], ["o1"], T.o1[:], T.cl[:])
+    tt(["fx2", "fy2"], ["d2f"], T.d2f[:], T.fx2[:], T.fy2[:], A.add)
+    ts(["d2f"], ["pmi"], T.pmi[:], T.d2f[:], 13, None, A.logical_shift_right)
+    ts(["pmi", "sgkt"], ["pm"], T.pm[:], T.pmi[:], s_, None, A.is_equal)
+    tt(["tauI", "o1", "pm"], ["gm"], T.gm[:], T.tauI[:, 0:512].indirect(T.o1[:, 0:16]), T.pm[:], A.mult)
+    for h in range(2):
+        mm("b%d" % (1 + h), T["b%d" % (1 + h)][:, 0:128], [(T.bone[:], T.gm[:, 128 * h:128 * h + 128], ["bone", "gm"])])
+    cp(["tauI"], ["tauU"], T.tauU[:], T.tauI[:])
+    idn(["dsc0"], ["dsc"], T.dsc[:], T.dsc[:], 1.0, -17.0 * 4096)
+    idn(["sgkt"], ["k16"], fc(8), k7, 1.0 / 16, 0.0)
+    act(["sgkt"], ["isA"], fc(9), t_, F.Relu, bias=1.0, scale=-1.0)
+    act(["sgkt"], ["alf"], fc(10), t_, F.Relu, bias=16.0, scale=-16.0)
+    act(["sgkt"], ["au"], fc(11), t_, F.Abs, bias=-2.0)
+    idn(["posN", "rowg"], ["lUa"], T.lU[:, 0:8], T.rowg[0:8, 0:8], 0.0, T.posN[:, 0:1])
+    idn(["posN", "rowg"], ["lUb"], T.lU[:, 8:32], T.rowg[0:8, 0:24], 0.0, T.posN[:, 1:2])
+    idn(["isA"], ["notA"], fc(12), fc(9), -1.0, 1.0)
+    idn(["isA"], ["nA128"], fc(13), fc(9), -1.0 / 128, 1.0 / 128)
+    idn(["isA"], ["nA16"], fc(14), fc(9), -1.0 / 16, 1.0 / 16)
+    idn(["isA"], ["nA8"], fc(15), fc(9), 1.0 / 8, -1.0 / 8)
+    act(["au"], ["e2"], fc(16), fc(11), F.Relu, bias=1.0, scale=-1.0)
+    idn(["alf"], ["bet"], fc(17), fc(10), -17.0, 16.0)
+    idn(["sgkt"], ["o8"], fc(18), t_, 8.0, -16.0)
+    idn(["sgkt", "nA16", "nA8"], ["c1"], fc(19), t_, fc(14), fc(15))
+    idn(["e2", "nA128"], ["c2"], fc(20), fc(16), -3.0 / 128, fc(13))
+    idn(["e2", "isA"], ["c0"], fc(21), fc(16), 1.0, fc(9))
+    idn(["o8", "notA"], ["o8n"], fc(22), fc(18), fc(12), 0.0)
+    idn(rowy + ["c1", "c2"], ["f1"], T.f1[:], T.rowy[:], fc(20, 32), fc(19, 32))
+
+    for h in range(2):
+        op("V", V.tensor_tensor_scan, ["dsc", "b%d" % (1 + h)], ["sc%d" % h], T.sc[:, 128 * h:128 * h + 128],
+           T.dsc[:, 128 * h:128 * h + 128], T["b%d" % (1 + h)][:, 0:128], 0.0, A.add, A.max)
+        ts(["sc%d" % h, "sub"], ["o2%d" % h], T.o2[:, 8 * h:8 * h + 8], T.sc[:, 128 * h + 15:128 * h + 128:16], fc(6), None, A.subtract)
+    ts(["rown", "s8"], ["zsel"], T.zsel[:], T.rown[:], fc(7), None, A.is_equal)
+    ts(rowo + ["sgkt"], ["enm"], T.enm[:], T.rowo[:], k7, None, A.is_equal)
+    Z = lambda i: T.zsel[:, 7 - i:135 - i]
+
+    cp(["tr0", "tr1", "o20"], ["x10"], T.x1[:, 0:128], T.trS[:].indirect(T.o2[:, 0:8]))
+    act(["tr0", "tr1", "o21"], ["x11"], T.x1[:, 128:256], T.trS[:].indirect(T.o2[:, 8:16]), F.Copy)
+    mm("b3", T.b3[:, 0:32], [(Z(i), T.x1[:, 32 * i:32 * i + 32], ["zsel", "x1%d" % (i // 4)]) for i in range(8)])
+    ts(["rown", "p"], ["iden"], T.iden[:], T.rown[:, 0:128], fc(0), None, A.is_equal)
+    tt(["f1"] + rowy, ["f2"], T.f2[:], T.f1[:], T.rowy[:], A.mult)
+    cp(["b3"], ["send1"], T.send1[:], T.b3[:, 0:32])
+
+    on = topo.engines(core, relays[0][0])
+    off = topo.engines(core, T.cores[same[0]])
+    rest = [e for e in on if e not in off]
+    slot = slice(32 * rank, 32 * rank + 32)
+    order_after("G", ["send1"], [])
+    g.remote_dma_fused([RemoteDMATransfer(dst_ids=[dst(topo, r, core)], dma_engine_mask=bits(e), remote_sem=sem.r1,
+                                          srcs=[T.send1[:]], dsts=[T.hop1[:]])
+                        for (r, _), e in zip(relays, (off, rest))], local_sem=sem.loc)
+    g.remote_dma_fused([RemoteDMATransfer(dst_ids=[dst(topo, T.cores[q], core) for q in same], dma_engine_mask=bits(off),
+                                          remote_sem=sem.a1d, srcs=[T.send1[:]], dsts=[T.land1[:, slot] for q in same])],
+                       local_sem=sem.loc)
+    wrote["land1d"] = ("a1d", len(same) * len(off))
+    wrote["land1x"] = ("a1x", len(cross) * len(off))
+    total["a1d"], total["a1x"] = wrote["land1d"][1], wrote["land1x"][1]
+
+    def compose(q, a, b):
+        src, out, keys = T.trS[:].indirect(T.tauU[:, a:b]), T.vt[:, 16 * a:16 * b], ["tr0", "tr1", "tauU"]
+        if q == "S":
+            act(keys, ["vt%d" % a], out, src, F.Copy)
+        else:
+            cp(keys, ["vt%d" % a], out, src)
+    compose("S", 256, 512)
+    mm("b0", T.b0[0:32, 4:5], [(T.enm[:], fc(8), ["enm", "k16"])])
+    ts(["b0"], ["k32"], fc(23, 32), T.b0[0:32, 4:5], 32.0, None, A.mult)
+    mm("b0", T.b0[0:32, 8:136], [(T.lU[:], T.expd[:], ["lUa", "lUb", "expd"])])
+    ts(colp + ["sgkt"], ["dlt"], T.dlt[:], T.colp[:], T.cF[0:32, 3:4], None, A.is_equal)
+    ts(["f2", "c0"], ["f3"], T.f3[:], T.f2[:], fc(21, 32), None, A.add)
+    ts(["k32", "o8n", "notA"], ["off"], fc(24, 32), fc(23, 32), fc(12, 32), fc(22, 32), A.mult, A.add)
+    tt(["f3", "dlt"], ["rr"], T.rr[:], T.f3[:], T.dlt[:], A.mult)
+    ts(["rowm", "isA", "off"], ["su"], T.su[:], T.rowm[:], fc(9, 32), fc(24, 32), A.mult, A.add)
+    tt(["b0", "su"], ["uU"], T.uU[:], T.b0[0:32, 8:136], T.su[:], A.add)
+    compose("V", 0, CUT)
+    if CUT < 256:
+        compose("S", CUT, 256)
+    table = ["vt0", "vt256"] + (["vt%d" % CUT] if CUT < 256 else [])
+
+    def sumup(key, land, own, ownkeys, name):
+        L = lambda q: land[:, 32 * q:32 * q + 32]
+        parts = [(T.iden[:], own, ["iden"] + ownkeys)] + [(T.iden[:], L(q), [name + "d"]) for q in same]
+        parts += [(T.iden[:], L(q), [name + "x"]) for q in cross]
+        mm(key, T[key][:, 0:32], parts)
+    sumup("b4", T.land1, T.send1[:], ["send1"], "land1")
+    act(["b4"], ["asq"], T.asq[:], T.b4[:, 0:32], F.Square)
+    mm("b5", T.b5[0:32, 0:32], [(T.enm[:], T.asq[:], ["enm", "asq"])])
+    op("V", V.tensor_tensor_scan, ["b5", "zero"], ["rmx"], T.rmx[:], T.b5[0:32, 0:32], T.zero[:], 0.0, A.max, A.max)
+    act(["rmx"], ["sgn", "cc"], T.sgn[:], T.rmx[:], F.Sign, bias=T.rmx[:, 31:32], scale=-1.0, accum_out=T.cc[:])
+    ts(["cc", "bet"], ["hb"], T.hb[:], T.cc[:], 15.5, fc(17, 32), A.is_ge, A.mult)
+    ts(["cc", "alf", "hb"], ["bb"], T.bb[:], T.cc[:], fc(10, 32), T.hb[:], A.mult, A.add)
+    act(["uU", "bb"], ["uq"], T.uq[:], T.uU[:], F.Square, bias=T.bb[:])
+    for h in range(2):
+        mm("b%d" % (6 + h), T["b%d" % (6 + h)][:, 0:64], [(T.uq[:], T.rr[:, 64 * h:64 * h + 64], ["uq", "rr"])])
+
+    def lists(h):
+        c = slice(64 * h, 64 * h + 64)
+        k = lambda n: n + str(h)
+        cp(["b%d" % (6 + h)], [k("d2i")], T.d2i[:, c], T["b%d" % (6 + h)][:, 0:64])
+        ts([k("d2i")], [k("t1")], T.t1[:, c], T.d2i[:, c], 8176, None, A.bitwise_and)
+        ts([k("d2i")], [k("t2")], T.t2[:, c], T.d2i[:, c], 13, None, A.logical_shift_right)
+        tt([k("t1"), k("t2")], [k("js")], T.js[:, c], T.t1[:, c], T.t2[:, c], A.add)
+        cp([k("js")], [k("o3")], T.o3[:, c], T.js[:, c])
+
+    def gather(P, q):
+        src = T.vt[:].indirect(T.o3[:, 32 * P:32 * P + 32])
+        out = T.x2[:, 512 * P:512 * P + 512]
+        keys = table + ["o3%d" % (P // 2)]
+        if q == "S":
+            act(keys, ["x2%d" % P], out, src, F.Copy)
+        else:
+            cp(keys, ["x2%d" % P], out, src)
+
+    bank = ["b1", "b2", "b3", "b0"]
+
+    def image(P):
+        mm(bank[P], T[bank[P]][:, 0:64], [(Z(i), T.x2[:, 512 * P + 64 * i:512 * P + 64 * i + 64], ["zsel", "x2%d" % P]) for i in range(8)])
+
+    def stow(P, q):
+        out = (T.sendAB if P < 2 else T.sendCD)[:, 64 * (P % 2):64 * (P % 2) + 64]
+        if q == "S":
+            act([bank[P]], ["send%d" % P], out, T[bank[P]][:, 0:64], F.Copy)
+        else:
+            cp([bank[P]], ["send%d" % P], out, T[bank[P]][:, 0:64])
+
+    lists(0)
+    gather(0, "S")
+    gather(1, "V")
+    image(0)
+    image(1)
+    lists(1)
+    stow(0, "S")
+    stow(1, "V")
+    gather(2, "S")
+    gather(3, "V")
+    image(2)
+    image(3)
+    stow(2, "S")
+    stow(3, "V")
+
+    for P, (r, dests) in enumerate(relays):
+        order_after("G", ["send%d" % P], [])
+        rid, pid = topo.addr(r, core)
+        g.remote_dma(T.hop2[:], T.sendAB[:, 64 * P:64 * P + 64], sem.r2, sem.loc, pid, rid, bits(on))
+    half = len(off) // 2
+    order_after("G", ["send2"], [])
+    g.remote_dma_fused([RemoteDMATransfer(dst_ids=[dst(topo, T.cores[q], core)], dma_engine_mask=bits(off[i * half:(i + 1) * half]),
+                                          remote_sem=sem.a2d, srcs=[T.sendCD[:, 32 * i:32 * i + 32]], dsts=[T.land2[:, slot]])
+                        for i, q in enumerate(same[:2])], local_sem=sem.loc)
+    order_after("G", ["send3"], [])
+    rid, pid = topo.addr(T.cores[same[2]], core)
+    g.remote_dma(T.land2[:, slot], T.sendCD[:, 64:96], sem.a2d, sem.loc, pid, rid, bits(off))
+    total["loc"] = len(on) + len(off) + 2 * len(on) + 2 * half + len(off)
+    a2d = 0
+    for q in same:
+        their = plan(T, topo, T.cores[q])[1]
+        a2d += half if their.index(rank) < 2 else len(off)
+    wrote["land2d"] = ("a2d", a2d)
+    wrote["land2x"] = ("a2x", len(cross) * half)
+    total["a2d"], total["a2x"] = a2d, len(cross) * half
+
+    ts(["rown", "k32"], ["prm0"], T.prm[:], T.rown[0:32, 0:8], 32.0, fc(23, 32), A.mult, A.is_equal)
+    ts(["prm0", "isA"], ["prm"], T.prm[:], T.prm[:], fc(9, 32), None, A.mult)
+    tt(["cc", "k32"], ["wc"], T.wc[:], T.cc[:], fc(23, 32), A.add)
+    mm("b5", T.b5[0:1, 0:8], [(T.wc[:], T.prm[:], ["wc", "prm"])])
+    cp(["b5"], ["wrow"], T.wrow[:], T.b5[0:1, 0:8])
+    dma("Y", "dw", T.w[:], T.wrow[:], ["wrow"], ["w"])
+
+    sumup("b4", T.land2, T.sendCD[:, 96:128], ["send3"], "land2")
+    cp(["b4"], ["yo"], T.yo[:], T.b4[:, 0:32])
+    dma("Y", "dy", T.y[:], T.yo[:], ["yo"], ["y"])
+    wait("Y", "dw", total["dw"])
+    wait("Y", "dy", total["dy"])
+    for name in sorted(total):
+        if max(known[q].get(name, 0) for q in eng) < total[name]:
+            wait("G", name, total[name])

@@ -1,17 +1,18 @@
 from concourse.bass import DstId, RemoteDMATransfer
 from concourse.mybir import AluOpType as A, ActivationFunctionType as F
 
+R = 2
 SB = {
     "float32": {"cF": [128, 40], "rowx": [128, 256], "rowb": [128, 256], "rowg": [128, 128], "rown": [128, 136], "rowm": [32, 128],
-                "rowo": [128, 32], "colp": [32, 128], "rowy": [32, 128], "zero": [32, 32], "bone": [128, 128], "dsc": [128, 256],
-                "enm": [128, 32], "uU": [32, 128], "su": [32, 128], "rr": [32, 128], "f1": [32, 128], "f2": [32, 128], "f3": [32, 128],
+                "rowo": [128, 32], "colp": [32, 128], "rowy": [32, 32], "zero": [32, 32], "bone": [128, 128], "dsc": [128, 256],
+                "enm": [128, 32], "uU": [32, 128], "su": [32, 128], "rr": [32, 128], "f1": [32, 32], "f2": [32, 32], "f3": [32, 32],
                 "dlt": [32, 128], "prm": [32, 8], "xy": [128, 2], "dx2": [128, 1], "dy2": [128, 16], "fx2": [128, 256],
                 "fy2": [128, 256], "pm": [128, 256], "gm": [128, 256], "sc": [128, 256], "asq": [128, 32], "rmx": [32, 32],
                 "sgn": [32, 32], "cc": [32, 1], "hb": [32, 1], "bb": [32, 1], "uq": [32, 128], "wc": [32, 1], "wrow": [1, 8],
                 "yo": [128, 32]},
     "bfloat16": {"trS": [128, 4096], "expd": [8, 128], "zsel": [128, 136], "iden": [128, 128], "posN": [8, 2], "lU": [8, 32],
                  "x1": [128, 256], "send1": [128, 32], "land1": [128, 256], "hop1": [128, 32], "vt": [128, 8192], "x2": [128, 2048],
-                 "sendAB": [128, 128], "sendCD": [128, 128], "hop2": [128, 64], "land2": [128, 256]},
+                 "sendAB": [128, 128], "sendCD": [128, 128], "hop2": [128, 128 // R], "land2": [128, 256]},
     "int32": {"posI": [8, 2], "tauI": [128, 512], "ip": [128, 1], "cI": [128, 4], "d2l": [128, 16], "cl": [128, 16], "d2f": [128, 256],
               "pmi": [128, 256], "d2i": [128, 128], "t1": [128, 128], "t2": [128, 128], "js": [128, 128]},
     "uint16": {"o1": [128, 16], "o2": [128, 16], "tauU": [128, 512], "o3": [128, 128]},
@@ -19,7 +20,7 @@ SB = {
 SCRATCH = {n: ("sbuf", s, d) for d, b in SB.items() for n, s in b.items()}
 SCRATCH.update({"b%d" % i: ("psum", [128, 512], "float32") for i in range(8)})
 SEMAPHORES = ["cV", "cS", "cP", "cG", "dpos", "dtau", "dtr", "dw", "dy", "a1d", "a1x", "a2d", "a2x", "r1", "r2", "loc"]
-CUT = 224
+CV, GV, GS = 222, 232, (232, 236, 240, 256)
 
 
 def bits(engines):
@@ -30,10 +31,17 @@ def plan(T, topo, src):
     me = T.rank_of(src)
     cross = [q for q, c in enumerate(T.cores) if not topo.may_write(src, c)]
     same = [q for q, c in enumerate(T.cores) if q != me and q not in cross]
-    relays = [c for c in topo.cores_of(src) if c != src and topo.die(c) == topo.die(src)
-              and all(topo.may_write(c, T.cores[q]) for q in cross)]
-    part = len(cross) // len(relays)
+    relays = [c for c in topo.cores_of(src) if c != src and all(topo.may_write(c, T.cores[q]) for q in cross)]
+    relays = sorted(relays, key=lambda c: topo.die(c) != topo.die(src))[:R]
+    part = len(cross) // R
     return cross, same, [(c, cross[i * part:(i + 1) * part]) for i, c in enumerate(relays)]
+
+
+def direct(T, topo, src):
+    me = T.rank_of(src)
+    cross, same, _ = plan(T, topo, src)
+    order = cross + sorted(same + [me])
+    return order, [[q for q in order[2 * P:2 * P + 2] if q != me] for P in (2, 3)]
 
 
 def dst(topo, d, src):
@@ -41,20 +49,29 @@ def dst(topo, d, src):
     return DstId(rid=rid, pnc=pid)
 
 
+def write(g, topo, core, parts, remote_sem, local_sem):
+    if len(parts) == 1:
+        d, out, src, e = parts[0]
+        rid, pid = topo.addr(d, core)
+        g.remote_dma(out, src, remote_sem, local_sem, pid, rid, bits(e))
+    else:
+        g.remote_dma_fused([RemoteDMATransfer(dst_ids=[dst(topo, d, core)], dma_engine_mask=bits(e), remote_sem=remote_sem,
+                                              srcs=[src], dsts=[out]) for d, out, src, e in parts], local_sem=local_sem)
+
+
 def relay_program(g, core, T, topo, rank, dests):
     sem = T.sem
     on = topo.engines(T.cores[rank], core)
     eng = topo.engines(core, T.cores[dests[0]])
-    half = len(eng) // 2
+    n = len(eng) // len(dests)
     slot = slice(32 * rank, 32 * rank + 32)
     to = [dst(topo, T.cores[q], core) for q in dests]
-    g.wait_ge(sem.r1, len(on) // 2)
+    g.wait_ge(sem.r1, len(on) // R)
     g.remote_dma_fused([RemoteDMATransfer(dst_ids=to, dma_engine_mask=bits(eng), remote_sem=sem.a1x, srcs=[T.hop1[:]],
                                           dsts=[T.land1[:, slot] for _ in to])], local_sem=sem.loc)
-    g.wait_ge(sem.r2, len(on))
-    g.remote_dma_fused([RemoteDMATransfer(dst_ids=[to[i]], dma_engine_mask=bits(eng[i * half:(i + 1) * half]), remote_sem=sem.a2x,
-                                          srcs=[T.hop2[:, 32 * i:32 * i + 32]], dsts=[T.land2[:, slot]])
-                        for i in range(len(to))], local_sem=sem.loc)
+    g.wait_ge(sem.r2, 2 * len(on) // R)
+    write(g, topo, core, [(T.cores[q], T.land2[:, slot], T.hop2[:, 32 * i:32 * i + 32], eng[i * n:(i + 1) * n])
+                          for i, q in enumerate(dests)], sem.a2x, sem.loc)
     g.wait_ge(sem.loc, 2 * len(eng))
 
 
@@ -67,7 +84,7 @@ def rank_program(g, core, T, topo):
                     relay_program(g, core, T, topo, q, dests)
         return
     cross, same, relays = plan(T, topo, core)
-    order = cross + same + [rank]
+    order, mine = direct(T, topo, core)
     sem = T.sem
     eng = {"G": g, "V": g.vector, "S": g.scalar, "P": g.tensor, "Y": g.sync}
     total = {}
@@ -107,11 +124,13 @@ def rank_program(g, core, T, topo):
         order_after(q, reads, writes)
         done(eng[q].dma_start(out, in_), name, 16, reads, writes)
 
-    def mm(key, out, parts):
+    def mm(key, out, parts, start=True, stop=True):
         for i, (l, r, keys) in enumerate(parts):
-            order_after("P", keys, [key] if i == 0 else [])
-            ins = g.tensor.matmul(out, l, r, i == 0, i == len(parts) - 1)
-        done(ins, "cP", 1, [k for p in parts for k in p[2]], [key])
+            a, z = start and i == 0, stop and i == len(parts) - 1
+            order_after("P", keys, [key] if a else [])
+            ins = g.tensor.matmul(out, l, r, a, z)
+        if stop:
+            done(ins, "cP", 1, [k for p in parts for k in p[2]], [key])
 
     V, S = g.vector, g.scalar
     ts = lambda reads, writes, *a: op("V", V.tensor_scalar, reads, writes, *a)
@@ -131,17 +150,22 @@ def rank_program(g, core, T, topo):
     op("G", g.iota, [], ["ip"], T.ip[:], [[0, 1]], 0, 1)
     iota("p", fc(0), [[0, 1]], 0, 1)
     iota("rowg", T.rowg[:], [[1, 8], [0, 16]], 0, 0)
+    b, h4, h1 = order[0], order[4] - order[0], order[1] - order[0]
+    if all(order[i] == b + (i // 4) * h4 + (i % 4) * h1 for i in range(8)):
+        iota("rowo0", T.rowo[:], [[0, 4], [h4, 2], [h1, 4]], b, 0)
+        rowo = ["rowo0"]
+    else:
+        for i, k in enumerate(order):
+            iota("rowo%d" % i, T.rowo[:, i::8], [[0, 4]], k, 0)
+        rowo = ["rowo%d" % i for i in range(8)]
     iota("rowx", T.rowx[:], [[0, 16], [16, 16]], 8, 0)
     iota("rowb", T.rowb[:], [[16, 16], [0, 16]], 8, 0)
     iota("rown", T.rown[:], [[1, 136]], 0, 0)
-    for P in range(4):
-        iota("rowy%d" % P, T.rowy[:, 32 * P:32 * P + 32], [[2, 8], [0, 2], [1, 2]], 0, 0)
+    iota("rowy", T.rowy[:], [[2, 8], [0, 2], [1, 2]], 0, 0)
     iota("rowm", T.rowm[:], [[0, 8], [1, 16]], 0, 0)
-    for i, k in enumerate(order):
-        iota("rowo%d" % i, T.rowo[:, i::8], [[0, 4]], k, 0)
     for P in range(4):
         iota("colp%d" % P, T.colp[:, 32 * P:32 * P + 32], [[0, 8], [1, 2], [0, 2]], 2 * P, 0)
-    rowy, rowo, colp = ["rowy%d" % P for P in range(4)], ["rowo%d" % i for i in range(8)], ["colp%d" % P for P in range(4)]
+    colp = ["colp%d" % P for P in range(4)]
 
     ts(["ip"], ["i0"], T.cI[:, 0:1], T.ip[:], 15, None, A.bitwise_and)
     ts(["ip"], ["i1"], T.cI[:, 1:2], T.ip[:], 4, None, A.logical_shift_right)
@@ -149,102 +173,115 @@ def rank_program(g, core, T, topo):
     ts(["ip"], ["i3"], T.cI[:, 3:4], T.ip[:], 3, None, A.logical_shift_right)
     cp(["i0", "i1", "i2", "i3"], ["sgkt"], T.cF[:, 1:5], T.cI[:])
     s_, g_, k7, t_ = fc(1), fc(2), fc(3), fc(4)
-    ts(["rowg", "p"], ["expd"], T.expd[:], T.rowg[0:8, :], fc(0, 8), None, A.is_equal)
     idn(["sgkt"], ["c16"], fc(5), s_, 16.0, 8.0)
-    idn(["sgkt"], ["sub"], fc(6), s_, -4096.0, 15.0 * 4096)
+    idn(["sgkt"], ["k16"], fc(8), k7, 1.0 / 16, 0.0)
     idn(["sgkt"], ["s8"], fc(7), s_, 8.0, 7.0)
+    idn(["sgkt"], ["sub"], fc(6), s_, -4096.0, 15.0 * 4096)
+    act(["sgkt"], ["isA"], fc(9), t_, F.Relu, bias=1.0, scale=-1.0)
+    act(["sgkt"], ["au"], fc(11), t_, F.Abs, bias=-2.0)
+    act(["sgkt"], ["alf"], fc(10), t_, F.Relu, bias=16.0, scale=-16.0)
+    idn(["isA"], ["nA128"], fc(13), fc(9), -1.0 / 128, 1.0 / 128)
+    act(["au"], ["e2"], fc(16), fc(11), F.Relu, bias=1.0, scale=-1.0)
+    idn(["isA"], ["nA16"], fc(14), fc(9), -1.0 / 16, 1.0 / 16)
+    idn(["isA"], ["nA8"], fc(15), fc(9), 1.0 / 8, -1.0 / 8)
+    idn(["isA"], ["notA"], fc(12), fc(9), -1.0, 1.0)
+    idn(["e2", "nA128"], ["c2"], fc(20), fc(16), -3.0 / 128, fc(13))
+    ts(["rowg", "p"], ["expd"], T.expd[:], T.rowg[0:8, :], fc(0, 8), None, A.is_equal)
     ts(["rowg", "sgkt"], ["bone"], T.bone[:], T.rowg[:], g_, None, A.is_equal)
     op("V", V.memset, [], ["zero"], T.zero[:], 0.0)
+    ts(rowo + ["sgkt"], ["enm"], T.enm[:], T.rowo[:], k7, None, A.is_equal)
 
     ts(["posI"], ["posN"], T.posN[:], T.posI[:], -1, None, A.mult)
     mm("b0", T.b0[:, 0:2], [(T.expd[:], T.posN[:], ["expd", "posN"])])
-    ts(["rowx", "c16"], ["dsc0"], T.dsc[:], T.rowx[:], fc(5), 18.0 * 4096, A.is_gt, A.mult)
     cp(["b0"], ["xy"], T.xy[:], T.b0[:, 0:2])
     nX, nY = T.xy[:, 0:1], T.xy[:, 1:2]
+    mm("b0", T.b0[0:32, 4:5], [(T.enm[:], fc(8), ["enm", "k16"])])
     act(["c16", "xy"], ["dx2"], T.dx2[:], fc(5), F.Square, bias=nX)
     act(["rowx", "xy"], ["dy2"], T.dy2[:], T.rowx[:, 0:16], F.Square, bias=nY)
-    act(["rowx", "xy"], ["fx2"], T.fx2[:], T.rowx[:], F.Square, bias=nX)
-    act(["rowb", "xy"], ["fy2"], T.fy2[:], T.rowb[:], F.Square, bias=nY)
-    ts(["dy2", "dx2"], ["d2l"], T.d2l[:], T.dy2[:], T.dx2[:], None, A.add)
-    ts(["d2l"], ["cl"], T.cl[:], T.d2l[:], 4, 511, A.logical_shift_right, A.bitwise_and)
-    cp(["cl"], ["o1"], T.o1[:], T.cl[:])
-    tt(["fx2", "fy2"], ["d2f"], T.d2f[:], T.fx2[:], T.fy2[:], A.add)
-    ts(["d2f"], ["pmi"], T.pmi[:], T.d2f[:], 13, None, A.logical_shift_right)
-    ts(["pmi", "sgkt"], ["pm"], T.pm[:], T.pmi[:], s_, None, A.is_equal)
-    tt(["tauI", "o1", "pm"], ["gm"], T.gm[:], T.tauI[:, 0:512].indirect(T.o1[:, 0:16]), T.pm[:], A.mult)
+    H = lambda t, h: T[t][:, 128 * h:128 * h + 128]
     for h in range(2):
-        mm("b%d" % (1 + h), T["b%d" % (1 + h)][:, 0:128], [(T.bone[:], T.gm[:, 128 * h:128 * h + 128], ["bone", "gm"])])
-    cp(["tauI"], ["tauU"], T.tauU[:], T.tauI[:])
+        act(["rowx", "xy"], ["fx2%d" % h], H("fx2", h), H("rowx", h), F.Square, bias=nX)
+        act(["rowb", "xy"], ["fy2%d" % h], H("fy2", h), H("rowb", h), F.Square, bias=nY)
+    k = lambda n, h: n + str(h)
+    ts(["rowx", "c16"], ["dsc0"], T.dsc[:], T.rowx[:], fc(5), 18.0 * 4096, A.is_gt, A.mult)
+    ts(["dy2", "dx2"], ["d2l"], T.d2l[:], T.dy2[:], T.dx2[:], None, A.add)
+    tt(["fx20", "fy20"], ["d2f0"], H("d2f", 0), H("fx2", 0), H("fy2", 0), A.add)
+    ts(["d2l"], ["cl"], T.cl[:], T.d2l[:], 4, 511, A.logical_shift_right, A.bitwise_and)
+    tt(["fx21", "fy21"], ["d2f1"], H("d2f", 1), H("fx2", 1), H("fy2", 1), A.add)
+    ts(["d2f0"], ["pmi0"], H("pmi", 0), H("d2f", 0), 13, None, A.logical_shift_right)
+    cp(["cl"], ["o1"], T.o1[:], T.cl[:])
+    ts(["d2f1"], ["pmi1"], H("pmi", 1), H("d2f", 1), 13, None, A.logical_shift_right)
+    for h in range(2):
+        ts([k("pmi", h), "sgkt"], [k("pm", h)], H("pm", h), H("pmi", h), s_, None, A.is_equal)
+    for h in range(2):
+        tt(["tauI", "o1", k("pm", h)], [k("gm", h)], H("gm", h), T.tauI[:, 0:512].indirect(T.o1[:, 8 * h:8 * h + 8]), H("pm", h), A.mult)
+        mm("b%d" % (1 + h), T["b%d" % (1 + h)][:, 0:128], [(T.bone[:], H("gm", h), ["bone", k("gm", h)])])
     idn(["dsc0"], ["dsc"], T.dsc[:], T.dsc[:], 1.0, -17.0 * 4096)
-    idn(["sgkt"], ["k16"], fc(8), k7, 1.0 / 16, 0.0)
-    act(["sgkt"], ["isA"], fc(9), t_, F.Relu, bias=1.0, scale=-1.0)
-    act(["sgkt"], ["alf"], fc(10), t_, F.Relu, bias=16.0, scale=-16.0)
-    act(["sgkt"], ["au"], fc(11), t_, F.Abs, bias=-2.0)
+    idn(["sgkt", "nA16", "nA8"], ["c1"], fc(19), t_, fc(14), fc(15))
+    idn(["sgkt"], ["o8"], fc(18), t_, 8.0, -16.0)
+    idn(["e2", "isA"], ["c0"], fc(21), fc(16), 1.0, fc(9))
+    idn(["rowy", "c1", "c2"], ["f1"], T.f1[:], T.rowy[:], fc(20, 32), fc(19, 32))
+    idn(["o8", "notA"], ["o8n"], fc(22), fc(18), fc(12), 0.0)
     idn(["posN", "rowg"], ["lUa"], T.lU[:, 0:8], T.rowg[0:8, 0:8], 0.0, T.posN[:, 0:1])
     idn(["posN", "rowg"], ["lUb"], T.lU[:, 8:32], T.rowg[0:8, 0:24], 0.0, T.posN[:, 1:2])
-    idn(["isA"], ["notA"], fc(12), fc(9), -1.0, 1.0)
-    idn(["isA"], ["nA128"], fc(13), fc(9), -1.0 / 128, 1.0 / 128)
-    idn(["isA"], ["nA16"], fc(14), fc(9), -1.0 / 16, 1.0 / 16)
-    idn(["isA"], ["nA8"], fc(15), fc(9), 1.0 / 8, -1.0 / 8)
-    act(["au"], ["e2"], fc(16), fc(11), F.Relu, bias=1.0, scale=-1.0)
+    idn(["b0"], ["k32"], fc(23, 32), T.b0[0:32, 4:5], 32.0, 0.0)
     idn(["alf"], ["bet"], fc(17), fc(10), -17.0, 16.0)
-    idn(["sgkt"], ["o8"], fc(18), t_, 8.0, -16.0)
-    idn(["sgkt", "nA16", "nA8"], ["c1"], fc(19), t_, fc(14), fc(15))
-    idn(["e2", "nA128"], ["c2"], fc(20), fc(16), -3.0 / 128, fc(13))
-    idn(["e2", "isA"], ["c0"], fc(21), fc(16), 1.0, fc(9))
-    idn(["o8", "notA"], ["o8n"], fc(22), fc(18), fc(12), 0.0)
-    idn(rowy + ["c1", "c2"], ["f1"], T.f1[:], T.rowy[:], fc(20, 32), fc(19, 32))
+    idn(["k32", "notA", "o8n"], ["off"], fc(24, 32), fc(23, 32), fc(12, 32), fc(22, 32))
+    mm("b0", T.b0[0:32, 8:136], [(T.lU[:], T.expd[:], ["lUa", "lUb", "expd"])])
 
-    for h in range(2):
-        op("V", V.tensor_tensor_scan, ["dsc", "b%d" % (1 + h)], ["sc%d" % h], T.sc[:, 128 * h:128 * h + 128],
-           T.dsc[:, 128 * h:128 * h + 128], T["b%d" % (1 + h)][:, 0:128], 0.0, A.add, A.max)
+    def scan(h):
+        op("V", V.tensor_tensor_scan, ["dsc", "b%d" % (1 + h)], ["sc%d" % h], H("sc", h), H("dsc", h),
+           T["b%d" % (1 + h)][:, 0:128], 0.0, A.add, A.max)
+
+    def pick(h):
         ts(["sc%d" % h, "sub"], ["o2%d" % h], T.o2[:, 8 * h:8 * h + 8], T.sc[:, 128 * h + 15:128 * h + 128:16], fc(6), None, A.subtract)
+    cp(["tauI"], ["tauU"], T.tauU[:], T.tauI[:])
+    scan(0)
     ts(["rown", "s8"], ["zsel"], T.zsel[:], T.rown[:], fc(7), None, A.is_equal)
-    ts(rowo + ["sgkt"], ["enm"], T.enm[:], T.rowo[:], k7, None, A.is_equal)
+    pick(0)
+    scan(1)
+    tt(["f1", "rowy"], ["f2"], T.f2[:], T.f1[:], T.rowy[:], A.mult)
+    pick(1)
     Z = lambda i: T.zsel[:, 7 - i:135 - i]
 
     cp(["tr0", "tr1", "o20"], ["x10"], T.x1[:, 0:128], T.trS[:].indirect(T.o2[:, 0:8]))
     act(["tr0", "tr1", "o21"], ["x11"], T.x1[:, 128:256], T.trS[:].indirect(T.o2[:, 8:16]), F.Copy)
     mm("b3", T.b3[:, 0:32], [(Z(i), T.x1[:, 32 * i:32 * i + 32], ["zsel", "x1%d" % (i // 4)]) for i in range(8)])
+    ts(colp + ["sgkt"], ["dlt"], T.dlt[:], T.colp[:], T.cF[0:32, 3:4], None, A.is_equal)
+    ts(["f2", "c0"], ["f3"], T.f3[:], T.f2[:], fc(21, 32), None, A.add)
     ts(["rown", "p"], ["iden"], T.iden[:], T.rown[:, 0:128], fc(0), None, A.is_equal)
-    tt(["f1"] + rowy, ["f2"], T.f2[:], T.f1[:], T.rowy[:], A.mult)
     cp(["b3"], ["send1"], T.send1[:], T.b3[:, 0:32])
 
     on = topo.engines(core, relays[0][0])
     off = topo.engines(core, T.cores[same[0]])
-    rest = [e for e in on if e not in off]
     slot = slice(32 * rank, 32 * rank + 32)
     order_after("G", ["send1"], [])
-    g.remote_dma_fused([RemoteDMATransfer(dst_ids=[dst(topo, r, core)], dma_engine_mask=bits(e), remote_sem=sem.r1,
-                                          srcs=[T.send1[:]], dsts=[T.hop1[:]])
-                        for (r, _), e in zip(relays, (off, rest))], local_sem=sem.loc)
+    n = len(on) // R
+    write(g, topo, core, [(r, T.hop1[:], T.send1[:], on[i * n:(i + 1) * n]) for i, (r, _) in enumerate(relays)], sem.r1, sem.loc)
     g.remote_dma_fused([RemoteDMATransfer(dst_ids=[dst(topo, T.cores[q], core) for q in same], dma_engine_mask=bits(off),
                                           remote_sem=sem.a1d, srcs=[T.send1[:]], dsts=[T.land1[:, slot] for q in same])],
                        local_sem=sem.loc)
     wrote["land1d"] = ("a1d", len(same) * len(off))
     wrote["land1x"] = ("a1x", len(cross) * len(off))
     total["a1d"], total["a1x"] = wrote["land1d"][1], wrote["land1x"][1]
+    total["loc"] = len(on) + len(off)
+
+    table = []
 
     def compose(q, a, b):
         src, out, keys = T.trS[:].indirect(T.tauU[:, a:b]), T.vt[:, 16 * a:16 * b], ["tr0", "tr1", "tauU"]
+        table.append("vt%d" % a)
         if q == "S":
-            act(keys, ["vt%d" % a], out, src, F.Copy)
+            act(keys, table[-1:], out, src, F.Copy)
         else:
-            cp(keys, ["vt%d" % a], out, src)
+            cp(keys, table[-1:], out, src)
     compose("S", 256, 512)
-    mm("b0", T.b0[0:32, 4:5], [(T.enm[:], fc(8), ["enm", "k16"])])
-    ts(["b0"], ["k32"], fc(23, 32), T.b0[0:32, 4:5], 32.0, None, A.mult)
-    mm("b0", T.b0[0:32, 8:136], [(T.lU[:], T.expd[:], ["lUa", "lUb", "expd"])])
-    ts(colp + ["sgkt"], ["dlt"], T.dlt[:], T.colp[:], T.cF[0:32, 3:4], None, A.is_equal)
-    ts(["f2", "c0"], ["f3"], T.f3[:], T.f2[:], fc(21, 32), None, A.add)
-    ts(["k32", "o8n", "notA"], ["off"], fc(24, 32), fc(23, 32), fc(12, 32), fc(22, 32), A.mult, A.add)
-    tt(["f3", "dlt"], ["rr"], T.rr[:], T.f3[:], T.dlt[:], A.mult)
     ts(["rowm", "isA", "off"], ["su"], T.su[:], T.rowm[:], fc(9, 32), fc(24, 32), A.mult, A.add)
+    for P in range(4):
+        c = slice(32 * P, 32 * P + 32)
+        tt(["f3", "dlt"], ["rr%d" % P], T.rr[:, c], T.f3[:], T.dlt[:, c], A.mult)
     tt(["b0", "su"], ["uU"], T.uU[:], T.b0[0:32, 8:136], T.su[:], A.add)
-    compose("V", 0, CUT)
-    if CUT < 256:
-        compose("S", CUT, 256)
-    table = ["vt0", "vt256"] + (["vt%d" % CUT] if CUT < 256 else [])
+    compose("V", 0, CV)
 
     def sumup(key, land, own, ownkeys, name):
         L = lambda q: land[:, 32 * q:32 * q + 32]
@@ -254,36 +291,46 @@ def rank_program(g, core, T, topo):
     sumup("b4", T.land1, T.send1[:], ["send1"], "land1")
     act(["b4"], ["asq"], T.asq[:], T.b4[:, 0:32], F.Square)
     mm("b5", T.b5[0:32, 0:32], [(T.enm[:], T.asq[:], ["enm", "asq"])])
+    compose("S", GS[0], GS[1])
     op("V", V.tensor_tensor_scan, ["b5", "zero"], ["rmx"], T.rmx[:], T.b5[0:32, 0:32], T.zero[:], 0.0, A.max, A.max)
-    act(["rmx"], ["sgn", "cc"], T.sgn[:], T.rmx[:], F.Sign, bias=T.rmx[:, 31:32], scale=-1.0, accum_out=T.cc[:])
-    ts(["cc", "bet"], ["hb"], T.hb[:], T.cc[:], 15.5, fc(17, 32), A.is_ge, A.mult)
+    last = T.rmx[:, 31:32]
+    act(["rmx"], ["sgn", "cc"], T.sgn[:], T.rmx[:], F.Sign, bias=last, scale=-1.0, accum_out=T.cc[:])
+    compose("S", GS[1], GS[2])
+    ts(["rmx", "bet"], ["hb"], T.hb[:], T.rmx[:, 15:16], last, fc(17, 32), A.is_lt, A.mult)
     ts(["cc", "alf", "hb"], ["bb"], T.bb[:], T.cc[:], fc(10, 32), T.hb[:], A.mult, A.add)
+    compose("V", CV, GV)
     act(["uU", "bb"], ["uq"], T.uq[:], T.uU[:], F.Square, bias=T.bb[:])
+    compose("S", GS[2], GS[3])
     for h in range(2):
-        mm("b%d" % (6 + h), T["b%d" % (6 + h)][:, 0:64], [(T.uq[:], T.rr[:, 64 * h:64 * h + 64], ["uq", "rr"])])
+        mm("b%d" % (6 + h), T["b%d" % (6 + h)][:, 0:64], [(T.uq[:], T.rr[:, 64 * h:64 * h + 64], ["uq", "rr0", "rr1", "rr2", "rr3"])])
 
-    def lists(h):
+    def lists(h, steps):
         c = slice(64 * h, 64 * h + 64)
-        k = lambda n: n + str(h)
-        cp(["b%d" % (6 + h)], [k("d2i")], T.d2i[:, c], T["b%d" % (6 + h)][:, 0:64])
-        ts([k("d2i")], [k("t1")], T.t1[:, c], T.d2i[:, c], 8176, None, A.bitwise_and)
-        ts([k("d2i")], [k("t2")], T.t2[:, c], T.d2i[:, c], 13, None, A.logical_shift_right)
-        tt([k("t1"), k("t2")], [k("js")], T.js[:, c], T.t1[:, c], T.t2[:, c], A.add)
-        cp([k("js")], [k("o3")], T.o3[:, c], T.js[:, c])
+        if 0 in steps:
+            cp(["b%d" % (6 + h)], [k("d2i", h)], T.d2i[:, c], T["b%d" % (6 + h)][:, 0:64])
+        if 1 in steps:
+            ts([k("d2i", h)], [k("t1", h)], T.t1[:, c], T.d2i[:, c], 8176, None, A.bitwise_and)
+        if 2 in steps:
+            ts([k("d2i", h)], [k("t2", h)], T.t2[:, c], T.d2i[:, c], 13, None, A.logical_shift_right)
+        if 3 in steps:
+            tt([k("t1", h), k("t2", h)], [k("js", h)], T.js[:, c], T.t1[:, c], T.t2[:, c], A.add)
+        if 4 in steps:
+            cp([k("js", h)], [k("o3", h)], T.o3[:, c], T.js[:, c])
 
-    def gather(P, q):
-        src = T.vt[:].indirect(T.o3[:, 32 * P:32 * P + 32])
-        out = T.x2[:, 512 * P:512 * P + 512]
-        keys = table + ["o3%d" % (P // 2)]
+    def gather(P, q, a, b):
+        src = T.vt[:].indirect(T.o3[:, 32 * P + a:32 * P + b])
+        out = T.x2[:, 512 * P + 16 * a:512 * P + 16 * b]
+        keys, w = table + ["o3%d" % (P // 2)], ["x2%d" % (8 * P + i) for i in range(a // 4, b // 4)]
         if q == "S":
-            act(keys, ["x2%d" % P], out, src, F.Copy)
+            act(keys, w, out, src, F.Copy)
         else:
-            cp(keys, ["x2%d" % P], out, src)
+            cp(keys, w, out, src)
 
     bank = ["b1", "b2", "b3", "b0"]
 
-    def image(P):
-        mm(bank[P], T[bank[P]][:, 0:64], [(Z(i), T.x2[:, 512 * P + 64 * i:512 * P + 64 * i + 64], ["zsel", "x2%d" % P]) for i in range(8)])
+    def image(P, a, b):
+        mm(bank[P], T[bank[P]][:, 0:64], [(Z(i), T.x2[:, 512 * P + 64 * i:512 * P + 64 * i + 64], ["zsel", "x2%d" % (8 * P + i)])
+                                          for i in range(a, b)], a == 0, b == 8)
 
     def stow(P, q):
         out = (T.sendAB if P < 2 else T.sendCD)[:, 64 * (P % 2):64 * (P % 2) + 64]
@@ -292,50 +339,51 @@ def rank_program(g, core, T, topo):
         else:
             cp([bank[P]], ["send%d" % P], out, T[bank[P]][:, 0:64])
 
-    lists(0)
-    gather(0, "S")
-    gather(1, "V")
-    image(0)
-    image(1)
-    lists(1)
+    lists(0, (0, 1, 2, 3))
+    lists(1, (0,))
+    lists(0, (4,))
+    for a in (0, 16):
+        gather(0, "S", a, a + 16)
+        gather(1, "V", a, a + 16)
+        image(0, a // 4, a // 4 + 4)
+        image(1, a // 4, a // 4 + 4)
+    lists(1, (1, 2, 3, 4))
     stow(0, "S")
     stow(1, "V")
-    gather(2, "S")
-    gather(3, "V")
-    image(2)
-    image(3)
-    stow(2, "S")
-    stow(3, "V")
+    for P, q in ((2, "S"), (3, "V")):
+        gather(P, q, 0, 32)
+        image(P, 0, 8)
+        stow(P, q)
 
-    for P, (r, dests) in enumerate(relays):
+    w = 128 // R
+    for P in range(2):
+        rs = range(P * R // 2, (P + 1) * R // 2)
+        n = len(on) // len(rs)
         order_after("G", ["send%d" % P], [])
-        rid, pid = topo.addr(r, core)
-        g.remote_dma(T.hop2[:], T.sendAB[:, 64 * P:64 * P + 64], sem.r2, sem.loc, pid, rid, bits(on))
-    half = len(off) // 2
-    order_after("G", ["send2"], [])
-    g.remote_dma_fused([RemoteDMATransfer(dst_ids=[dst(topo, T.cores[q], core)], dma_engine_mask=bits(off[i * half:(i + 1) * half]),
-                                          remote_sem=sem.a2d, srcs=[T.sendCD[:, 32 * i:32 * i + 32]], dsts=[T.land2[:, slot]])
-                        for i, q in enumerate(same[:2])], local_sem=sem.loc)
-    order_after("G", ["send3"], [])
-    rid, pid = topo.addr(T.cores[same[2]], core)
-    g.remote_dma(T.land2[:, slot], T.sendCD[:, 64:96], sem.a2d, sem.loc, pid, rid, bits(off))
-    total["loc"] = len(on) + len(off) + 2 * len(on) + 2 * half + len(off)
-    a2d = 0
-    for q in same:
-        their = plan(T, topo, T.cores[q])[1]
-        a2d += half if their.index(rank) < 2 else len(off)
-    wrote["land2d"] = ("a2d", a2d)
-    wrote["land2x"] = ("a2x", len(cross) * half)
-    total["a2d"], total["a2x"] = a2d, len(cross) * half
+        write(g, topo, core, [(relays[r][0], T.hop2[:], T.sendAB[:, w * r:w * r + w], on[i * n:(i + 1) * n])
+                              for i, r in enumerate(rs)], sem.r2, sem.loc)
+        total["loc"] += len(on)
+    for P, qs in zip((2, 3), mine):
+        n = len(off) // len(qs)
+        order_after("G", ["send%d" % P], [])
+        at = [64 * (P - 2) + 32 * (order.index(q) % 2) for q in qs]
+        write(g, topo, core, [(T.cores[q], T.land2[:, slot], T.sendCD[:, c:c + 32], off[i * n:(i + 1) * n])
+                              for i, (q, c) in enumerate(zip(qs, at))], sem.a2d, sem.loc)
+        total["loc"] += n * len(qs)
+    total["a2d"] = sum(len(off) // len(qs) for q in same for qs in direct(T, topo, T.cores[q])[1] if rank in qs)
+    total["a2x"] = len(cross) * (len(off) // (len(cross) // R))
+    wrote["land2d"], wrote["land2x"] = ("a2d", total["a2d"]), ("a2x", total["a2x"])
 
     ts(["rown", "k32"], ["prm0"], T.prm[:], T.rown[0:32, 0:8], 32.0, fc(23, 32), A.mult, A.is_equal)
-    ts(["prm0", "isA"], ["prm"], T.prm[:], T.prm[:], fc(9, 32), None, A.mult)
     tt(["cc", "k32"], ["wc"], T.wc[:], T.cc[:], fc(23, 32), A.add)
+    ts(["prm0", "isA"], ["prm"], T.prm[:], T.prm[:], fc(9, 32), None, A.mult)
     mm("b5", T.b5[0:1, 0:8], [(T.wc[:], T.prm[:], ["wc", "prm"])])
     cp(["b5"], ["wrow"], T.wrow[:], T.b5[0:1, 0:8])
     dma("Y", "dw", T.w[:], T.wrow[:], ["wrow"], ["w"])
 
-    sumup("b4", T.land2, T.sendCD[:, 96:128], ["send3"], "land2")
+    i = order.index(rank)
+    c = 64 * (i // 2 - 2) + 32 * (i % 2)
+    sumup("b4", T.land2, T.sendCD[:, c:c + 32], ["send%d" % (i // 2)], "land2")
     cp(["b4"], ["yo"], T.yo[:], T.b4[:, 0:32])
     dma("Y", "dy", T.y[:], T.yo[:], ["yo"], ["y"])
     wait("Y", "dw", total["dw"])

from concourse.bass import DstId, RemoteDMATransfer
from concourse.mybir import AluOpType as A, ActivationFunctionType as F

R = 2
SB = {
    "float32": {"cF": [128, 40], "rowx": [128, 256], "rowb": [128, 256], "rowg": [128, 128], "rown": [128, 136], "rowm": [32, 128],
                "rowo": [128, 32], "colp": [32, 128], "rowy": [32, 32], "zero": [32, 32], "bone": [128, 128], "dsc": [128, 256],
                "enm": [128, 32], "uU": [32, 128], "su": [32, 128], "rr": [32, 128], "f1": [32, 32], "f2": [32, 32], "f3": [32, 32],
                "dlt": [32, 128], "prm": [32, 8], "xy": [128, 2], "dx2": [128, 1], "dy2": [128, 16], "fx2": [128, 256],
                "fy2": [128, 256], "pm": [128, 256], "gm": [128, 256], "sc": [128, 256], "asq": [128, 32], "rmx": [32, 32],
                "sgn": [32, 32], "cc": [32, 1], "hb": [32, 1], "bb": [32, 1], "uq": [32, 128], "wc": [32, 1], "wrow": [1, 8],
                "yo": [128, 32]},
    "bfloat16": {"trS": [128, 4096], "expd": [8, 128], "zsel": [128, 136], "iden": [128, 128], "posN": [8, 2], "lU": [8, 32],
                 "x1": [128, 256], "send1": [128, 32], "land1": [128, 256], "hop1": [128, 32], "vt": [128, 8192], "x2": [128, 2048],
                 "sendAB": [128, 128], "sendCD": [128, 128], "hop2": [128, 128 // R], "land2": [128, 256]},
    "int32": {"posI": [8, 2], "tauI": [128, 512], "ip": [128, 1], "cI": [128, 4], "d2l": [128, 16], "cl": [128, 16], "d2f": [128, 256],
              "pmi": [128, 256], "d2i": [128, 128], "t1": [128, 128], "t2": [128, 128], "js": [128, 128]},
    "uint16": {"o1": [128, 16], "o2": [128, 16], "tauU": [128, 512], "o3": [128, 128]},
}
SCRATCH = {n: ("sbuf", s, d) for d, b in SB.items() for n, s in b.items()}
SCRATCH.update({"b%d" % i: ("psum", [128, 512], "float32") for i in range(8)})
SEMAPHORES = ["cV", "cS", "cP", "cG", "dpos", "dtau", "dtr", "dw", "dy", "a1d", "a1x", "a2d", "a2x", "r1", "r2", "loc"]
CV, GV, GS = 222, 232, (232, 236, 240, 256)


def bits(engines):
    return sum(1 << e for e in engines)


def plan(T, topo, src):
    me = T.rank_of(src)
    cross = [q for q, c in enumerate(T.cores) if not topo.may_write(src, c)]
    same = [q for q, c in enumerate(T.cores) if q != me and q not in cross]
    relays = [c for c in topo.cores_of(src) if c != src and all(topo.may_write(c, T.cores[q]) for q in cross)]
    relays = sorted(relays, key=lambda c: topo.die(c) != topo.die(src))[:R]
    part = len(cross) // R
    return cross, same, [(c, cross[i * part:(i + 1) * part]) for i, c in enumerate(relays)]


def direct(T, topo, src):
    me = T.rank_of(src)
    cross, same, _ = plan(T, topo, src)
    order = cross + sorted(same + [me])
    return order, [[q for q in order[2 * P:2 * P + 2] if q != me] for P in (2, 3)]


def dst(topo, d, src):
    rid, pid = topo.addr(d, src)
    return DstId(rid=rid, pnc=pid)


def write(g, topo, core, parts, remote_sem, local_sem):
    if len(parts) == 1:
        d, out, src, e = parts[0]
        rid, pid = topo.addr(d, core)
        g.remote_dma(out, src, remote_sem, local_sem, pid, rid, bits(e))
    else:
        g.remote_dma_fused([RemoteDMATransfer(dst_ids=[dst(topo, d, core)], dma_engine_mask=bits(e), remote_sem=remote_sem,
                                              srcs=[src], dsts=[out]) for d, out, src, e in parts], local_sem=local_sem)


def relay_program(g, core, T, topo, rank, dests):
    sem = T.sem
    on = topo.engines(T.cores[rank], core)
    eng = topo.engines(core, T.cores[dests[0]])
    n = len(eng) // len(dests)
    slot = slice(32 * rank, 32 * rank + 32)
    to = [dst(topo, T.cores[q], core) for q in dests]
    g.wait_ge(sem.r1, len(on) // R)
    g.remote_dma_fused([RemoteDMATransfer(dst_ids=to, dma_engine_mask=bits(eng), remote_sem=sem.a1x, srcs=[T.hop1[:]],
                                          dsts=[T.land1[:, slot] for _ in to])], local_sem=sem.loc)
    g.wait_ge(sem.r2, 2 * len(on) // R)
    write(g, topo, core, [(T.cores[q], T.land2[:, slot], T.hop2[:, 32 * i:32 * i + 32], eng[i * n:(i + 1) * n])
                          for i, q in enumerate(dests)], sem.a2x, sem.loc)
    g.wait_ge(sem.loc, 2 * len(eng))


def rank_program(g, core, T, topo):
    rank = T.rank_of(core)
    if rank is None:
        for q, c in enumerate(T.cores):
            for r, dests in plan(T, topo, c)[2]:
                if r == core:
                    relay_program(g, core, T, topo, q, dests)
        return
    cross, same, relays = plan(T, topo, core)
    order, mine = direct(T, topo, core)
    sem = T.sem
    eng = {"G": g, "V": g.vector, "S": g.scalar, "P": g.tensor, "Y": g.sync}
    total = {}
    known = {q: {} for q in eng}
    wrote, read = {}, {}

    def wait(q, name, val):
        if known[q].get(name, 0) < val:
            eng[q].wait_ge(sem[name], val)
            known[q][name] = val

    def order_after(q, reads, writes):
        need = {}
        hs = [wrote[k] for k in reads + writes if k in wrote]
        for k in writes:
            hs += read.get(k, [])
        for name, val in hs:
            need[name] = max(need.get(name, 0), val)
        for name in sorted(need):
            wait(q, name, need[name])

    def done(ins, name, n, reads, writes):
        total[name] = total.get(name, 0) + n
        ins.then_inc(sem[name], n)
        h = (name, total[name])
        for k in reads:
            read.setdefault(k, []).append(h)
        for k in writes:
            wrote[k] = h
            read[k] = []

    def op(q, call, reads, writes, *args, **kw):
        order_after(q, reads, writes)
        done(call(*args, **kw), "c" + q, 1, reads, writes)

    def dma(q, name, out, in_, reads, writes):
        order_after(q, reads, writes)
        done(eng[q].dma_start(out, in_), name, 16, reads, writes)

    def mm(key, out, parts, start=True, stop=True):
        for i, (l, r, keys) in enumerate(parts):
            a, z = start and i == 0, stop and i == len(parts) - 1
            order_after("P", keys, [key] if a else [])
            ins = g.tensor.matmul(out, l, r, a, z)
        if stop:
            done(ins, "cP", 1, [k for p in parts for k in p[2]], [key])

    V, S = g.vector, g.scalar
    ts = lambda reads, writes, *a: op("V", V.tensor_scalar, reads, writes, *a)
    tt = lambda reads, writes, *a: op("V", V.tensor_tensor, reads, writes, *a)
    cp = lambda reads, writes, *a: op("V", V.tensor_copy, reads, writes, *a)
    act = lambda reads, writes, *a, **k: op("S", S.activation, reads, writes, *a, **k)
    idn = lambda reads, writes, out, in_, scale, bias: act(reads, writes, out, in_, F.Identity, bias=bias, scale=scale)
    iota = lambda w, out, pat, base, cm: op("G", g.iota, [], [w], out, pat, base, cm, allow_small_or_imprecise_dtypes=True)
    fc = lambda i, n=128: T.cF[0:n, i:i + 1]

    dma("Y", "dpos", T.posI[:], T.pos[:], [], ["posI"])
    dma("S", "dtau", T.tauI[:], T.tau[:], [], ["tauI"])
    dma("Y", "dtr", T.trS[0:64, :], T.tr[0:64, :], [], ["tr0"])
    dma("S", "dtr", T.trS[64:128, :], T.tr[64:128, :], [], ["tr1"])
    wrote["tr0"] = wrote["tr1"]

    op("G", g.iota, [], ["ip"], T.ip[:], [[0, 1]], 0, 1)
    iota("p", fc(0), [[0, 1]], 0, 1)
    iota("rowg", T.rowg[:], [[1, 8], [0, 16]], 0, 0)
    b, h4, h1 = order[0], order[4] - order[0], order[1] - order[0]
    if all(order[i] == b + (i // 4) * h4 + (i % 4) * h1 for i in range(8)):
        iota("rowo0", T.rowo[:], [[0, 4], [h4, 2], [h1, 4]], b, 0)
        rowo = ["rowo0"]
    else:
        for i, k in enumerate(order):
            iota("rowo%d" % i, T.rowo[:, i::8], [[0, 4]], k, 0)
        rowo = ["rowo%d" % i for i in range(8)]
    iota("rowx", T.rowx[:], [[0, 16], [16, 16]], 8, 0)
    iota("rowb", T.rowb[:], [[16, 16], [0, 16]], 8, 0)
    iota("rown", T.rown[:], [[1, 136]], 0, 0)
    iota("rowy", T.rowy[:], [[2, 8], [0, 2], [1, 2]], 0, 0)
    iota("rowm", T.rowm[:], [[0, 8], [1, 16]], 0, 0)
    for P in range(4):
        iota("colp%d" % P, T.colp[:, 32 * P:32 * P + 32], [[0, 8], [1, 2], [0, 2]], 2 * P, 0)
    colp = ["colp%d" % P for P in range(4)]

    ts(["ip"], ["i0"], T.cI[:, 0:1], T.ip[:], 15, None, A.bitwise_and)
    ts(["ip"], ["i1"], T.cI[:, 1:2], T.ip[:], 4, None, A.logical_shift_right)
    ts(["ip"], ["i2"], T.cI[:, 2:3], T.ip[:], 7, None, A.bitwise_and)
    ts(["ip"], ["i3"], T.cI[:, 3:4], T.ip[:], 3, None, A.logical_shift_right)
    cp(["i0", "i1", "i2", "i3"], ["sgkt"], T.cF[:, 1:5], T.cI[:])
    s_, g_, k7, t_ = fc(1), fc(2), fc(3), fc(4)
    idn(["sgkt"], ["c16"], fc(5), s_, 16.0, 8.0)
    idn(["sgkt"], ["k16"], fc(8), k7, 1.0 / 16, 0.0)
    idn(["sgkt"], ["s8"], fc(7), s_, 8.0, 7.0)
    idn(["sgkt"], ["sub"], fc(6), s_, -4096.0, 15.0 * 4096)
    act(["sgkt"], ["isA"], fc(9), t_, F.Relu, bias=1.0, scale=-1.0)
    act(["sgkt"], ["au"], fc(11), t_, F.Abs, bias=-2.0)
    act(["sgkt"], ["alf"], fc(10), t_, F.Relu, bias=16.0, scale=-16.0)
    idn(["isA"], ["nA128"], fc(13), fc(9), -1.0 / 128, 1.0 / 128)
    act(["au"], ["e2"], fc(16), fc(11), F.Relu, bias=1.0, scale=-1.0)
    idn(["isA"], ["nA16"], fc(14), fc(9), -1.0 / 16, 1.0 / 16)
    idn(["isA"], ["nA8"], fc(15), fc(9), 1.0 / 8, -1.0 / 8)
    idn(["isA"], ["notA"], fc(12), fc(9), -1.0, 1.0)
    idn(["e2", "nA128"], ["c2"], fc(20), fc(16), -3.0 / 128, fc(13))
    ts(["rowg", "p"], ["expd"], T.expd[:], T.rowg[0:8, :], fc(0, 8), None, A.is_equal)
    ts(["rowg", "sgkt"], ["bone"], T.bone[:], T.rowg[:], g_, None, A.is_equal)
    op("V", V.memset, [], ["zero"], T.zero[:], 0.0)
    ts(rowo + ["sgkt"], ["enm"], T.enm[:], T.rowo[:], k7, None, A.is_equal)

    ts(["posI"], ["posN"], T.posN[:], T.posI[:], -1, None, A.mult)
    mm("b0", T.b0[:, 0:2], [(T.expd[:], T.posN[:], ["expd", "posN"])])
    cp(["b0"], ["xy"], T.xy[:], T.b0[:, 0:2])
    nX, nY = T.xy[:, 0:1], T.xy[:, 1:2]
    mm("b0", T.b0[0:32, 4:5], [(T.enm[:], fc(8), ["enm", "k16"])])
    act(["c16", "xy"], ["dx2"], T.dx2[:], fc(5), F.Square, bias=nX)
    act(["rowx", "xy"], ["dy2"], T.dy2[:], T.rowx[:, 0:16], F.Square, bias=nY)
    H = lambda t, h: T[t][:, 128 * h:128 * h + 128]
    for h in range(2):
        act(["rowx", "xy"], ["fx2%d" % h], H("fx2", h), H("rowx", h), F.Square, bias=nX)
        act(["rowb", "xy"], ["fy2%d" % h], H("fy2", h), H("rowb", h), F.Square, bias=nY)
    k = lambda n, h: n + str(h)
    ts(["rowx", "c16"], ["dsc0"], T.dsc[:], T.rowx[:], fc(5), 18.0 * 4096, A.is_gt, A.mult)
    ts(["dy2", "dx2"], ["d2l"], T.d2l[:], T.dy2[:], T.dx2[:], None, A.add)
    tt(["fx20", "fy20"], ["d2f0"], H("d2f", 0), H("fx2", 0), H("fy2", 0), A.add)
    ts(["d2l"], ["cl"], T.cl[:], T.d2l[:], 4, 511, A.logical_shift_right, A.bitwise_and)
    tt(["fx21", "fy21"], ["d2f1"], H("d2f", 1), H("fx2", 1), H("fy2", 1), A.add)
    ts(["d2f0"], ["pmi0"], H("pmi", 0), H("d2f", 0), 13, None, A.logical_shift_right)
    cp(["cl"], ["o1"], T.o1[:], T.cl[:])
    ts(["d2f1"], ["pmi1"], H("pmi", 1), H("d2f", 1), 13, None, A.logical_shift_right)
    for h in range(2):
        ts([k("pmi", h), "sgkt"], [k("pm", h)], H("pm", h), H("pmi", h), s_, None, A.is_equal)
    for h in range(2):
        tt(["tauI", "o1", k("pm", h)], [k("gm", h)], H("gm", h), T.tauI[:, 0:512].indirect(T.o1[:, 8 * h:8 * h + 8]), H("pm", h), A.mult)
        mm("b%d" % (1 + h), T["b%d" % (1 + h)][:, 0:128], [(T.bone[:], H("gm", h), ["bone", k("gm", h)])])
    idn(["dsc0"], ["dsc"], T.dsc[:], T.dsc[:], 1.0, -17.0 * 4096)
    idn(["sgkt", "nA16", "nA8"], ["c1"], fc(19), t_, fc(14), fc(15))
    idn(["sgkt"], ["o8"], fc(18), t_, 8.0, -16.0)
    idn(["e2", "isA"], ["c0"], fc(21), fc(16), 1.0, fc(9))
    idn(["rowy", "c1", "c2"], ["f1"], T.f1[:], T.rowy[:], fc(20, 32), fc(19, 32))
    idn(["o8", "notA"], ["o8n"], fc(22), fc(18), fc(12), 0.0)
    idn(["posN", "rowg"], ["lUa"], T.lU[:, 0:8], T.rowg[0:8, 0:8], 0.0, T.posN[:, 0:1])
    idn(["posN", "rowg"], ["lUb"], T.lU[:, 8:32], T.rowg[0:8, 0:24], 0.0, T.posN[:, 1:2])
    idn(["b0"], ["k32"], fc(23, 32), T.b0[0:32, 4:5], 32.0, 0.0)
    idn(["alf"], ["bet"], fc(17), fc(10), -17.0, 16.0)
    idn(["k32", "notA", "o8n"], ["off"], fc(24, 32), fc(23, 32), fc(12, 32), fc(22, 32))
    mm("b0", T.b0[0:32, 8:136], [(T.lU[:], T.expd[:], ["lUa", "lUb", "expd"])])

    def scan(h):
        op("V", V.tensor_tensor_scan, ["dsc", "b%d" % (1 + h)], ["sc%d" % h], H("sc", h), H("dsc", h),
           T["b%d" % (1 + h)][:, 0:128], 0.0, A.add, A.max)

    def pick(h):
        ts(["sc%d" % h, "sub"], ["o2%d" % h], T.o2[:, 8 * h:8 * h + 8], T.sc[:, 128 * h + 15:128 * h + 128:16], fc(6), None, A.subtract)
    cp(["tauI"], ["tauU"], T.tauU[:], T.tauI[:])
    scan(0)
    ts(["rown", "s8"], ["zsel"], T.zsel[:], T.rown[:], fc(7), None, A.is_equal)
    pick(0)
    scan(1)
    tt(["f1", "rowy"], ["f2"], T.f2[:], T.f1[:], T.rowy[:], A.mult)
    pick(1)
    Z = lambda i: T.zsel[:, 7 - i:135 - i]

    cp(["tr0", "tr1", "o20"], ["x10"], T.x1[:, 0:128], T.trS[:].indirect(T.o2[:, 0:8]))
    act(["tr0", "tr1", "o21"], ["x11"], T.x1[:, 128:256], T.trS[:].indirect(T.o2[:, 8:16]), F.Copy)
    mm("b3", T.b3[:, 0:32], [(Z(i), T.x1[:, 32 * i:32 * i + 32], ["zsel", "x1%d" % (i // 4)]) for i in range(8)])
    ts(colp + ["sgkt"], ["dlt"], T.dlt[:], T.colp[:], T.cF[0:32, 3:4], None, A.is_equal)
    ts(["f2", "c0"], ["f3"], T.f3[:], T.f2[:], fc(21, 32), None, A.add)
    ts(["rown", "p"], ["iden"], T.iden[:], T.rown[:, 0:128], fc(0), None, A.is_equal)
    cp(["b3"], ["send1"], T.send1[:], T.b3[:, 0:32])

    on = topo.engines(core, relays[0][0])
    off = topo.engines(core, T.cores[same[0]])
    slot = slice(32 * rank, 32 * rank + 32)
    order_after("G", ["send1"], [])
    n = len(on) // R
    write(g, topo, core, [(r, T.hop1[:], T.send1[:], on[i * n:(i + 1) * n]) for i, (r, _) in enumerate(relays)], sem.r1, sem.loc)
    g.remote_dma_fused([RemoteDMATransfer(dst_ids=[dst(topo, T.cores[q], core) for q in same], dma_engine_mask=bits(off),
                                          remote_sem=sem.a1d, srcs=[T.send1[:]], dsts=[T.land1[:, slot] for q in same])],
                       local_sem=sem.loc)
    wrote["land1d"] = ("a1d", len(same) * len(off))
    wrote["land1x"] = ("a1x", len(cross) * len(off))
    total["a1d"], total["a1x"] = wrote["land1d"][1], wrote["land1x"][1]
    total["loc"] = len(on) + len(off)

    table = []

    def compose(q, a, b):
        src, out, keys = T.trS[:].indirect(T.tauU[:, a:b]), T.vt[:, 16 * a:16 * b], ["tr0", "tr1", "tauU"]
        table.append("vt%d" % a)
        if q == "S":
            act(keys, table[-1:], out, src, F.Copy)
        else:
            cp(keys, table[-1:], out, src)
    compose("S", 256, 512)
    ts(["rowm", "isA", "off"], ["su"], T.su[:], T.rowm[:], fc(9, 32), fc(24, 32), A.mult, A.add)
    for P in range(4):
        c = slice(32 * P, 32 * P + 32)
        tt(["f3", "dlt"], ["rr%d" % P], T.rr[:, c], T.f3[:], T.dlt[:, c], A.mult)
    tt(["b0", "su"], ["uU"], T.uU[:], T.b0[0:32, 8:136], T.su[:], A.add)
    compose("V", 0, CV)

    def sumup(key, land, own, ownkeys, name):
        L = lambda q: land[:, 32 * q:32 * q + 32]
        parts = [(T.iden[:], own, ["iden"] + ownkeys)] + [(T.iden[:], L(q), [name + "d"]) for q in same]
        parts += [(T.iden[:], L(q), [name + "x"]) for q in cross]
        mm(key, T[key][:, 0:32], parts)
    sumup("b4", T.land1, T.send1[:], ["send1"], "land1")
    act(["b4"], ["asq"], T.asq[:], T.b4[:, 0:32], F.Square)
    mm("b5", T.b5[0:32, 0:32], [(T.enm[:], T.asq[:], ["enm", "asq"])])
    compose("S", GS[0], GS[1])
    op("V", V.tensor_tensor_scan, ["b5", "zero"], ["rmx"], T.rmx[:], T.b5[0:32, 0:32], T.zero[:], 0.0, A.max, A.max)
    last = T.rmx[:, 31:32]
    act(["rmx"], ["sgn", "cc"], T.sgn[:], T.rmx[:], F.Sign, bias=last, scale=-1.0, accum_out=T.cc[:])
    compose("S", GS[1], GS[2])
    ts(["rmx", "bet"], ["hb"], T.hb[:], T.rmx[:, 15:16], last, fc(17, 32), A.is_lt, A.mult)
    ts(["cc", "alf", "hb"], ["bb"], T.bb[:], T.cc[:], fc(10, 32), T.hb[:], A.mult, A.add)
    compose("V", CV, GV)
    act(["uU", "bb"], ["uq"], T.uq[:], T.uU[:], F.Square, bias=T.bb[:])
    compose("S", GS[2], GS[3])
    for h in range(2):
        mm("b%d" % (6 + h), T["b%d" % (6 + h)][:, 0:64], [(T.uq[:], T.rr[:, 64 * h:64 * h + 64], ["uq", "rr0", "rr1", "rr2", "rr3"])])

    def lists(h, steps):
        c = slice(64 * h, 64 * h + 64)
        if 0 in steps:
            cp(["b%d" % (6 + h)], [k("d2i", h)], T.d2i[:, c], T["b%d" % (6 + h)][:, 0:64])
        if 1 in steps:
            ts([k("d2i", h)], [k("t1", h)], T.t1[:, c], T.d2i[:, c], 8176, None, A.bitwise_and)
        if 2 in steps:
            ts([k("d2i", h)], [k("t2", h)], T.t2[:, c], T.d2i[:, c], 13, None, A.logical_shift_right)
        if 3 in steps:
            tt([k("t1", h), k("t2", h)], [k("js", h)], T.js[:, c], T.t1[:, c], T.t2[:, c], A.add)
        if 4 in steps:
            cp([k("js", h)], [k("o3", h)], T.o3[:, c], T.js[:, c])

    def gather(P, q, a, b):
        src = T.vt[:].indirect(T.o3[:, 32 * P + a:32 * P + b])
        out = T.x2[:, 512 * P + 16 * a:512 * P + 16 * b]
        keys, w = table + ["o3%d" % (P // 2)], ["x2%d" % (8 * P + i) for i in range(a // 4, b // 4)]
        if q == "S":
            act(keys, w, out, src, F.Copy)
        else:
            cp(keys, w, out, src)

    bank = ["b1", "b2", "b3", "b0"]

    def image(P, a, b):
        mm(bank[P], T[bank[P]][:, 0:64], [(Z(i), T.x2[:, 512 * P + 64 * i:512 * P + 64 * i + 64], ["zsel", "x2%d" % (8 * P + i)])
                                          for i in range(a, b)], a == 0, b == 8)

    def stow(P, q):
        out = (T.sendAB if P < 2 else T.sendCD)[:, 64 * (P % 2):64 * (P % 2) + 64]
        if q == "S":
            act([bank[P]], ["send%d" % P], out, T[bank[P]][:, 0:64], F.Copy)
        else:
            cp([bank[P]], ["send%d" % P], out, T[bank[P]][:, 0:64])

    lists(0, (0, 1, 2, 3))
    lists(1, (0,))
    lists(0, (4,))
    for a in (0, 16):
        gather(0, "S", a, a + 16)
        gather(1, "V", a, a + 16)
        image(0, a // 4, a // 4 + 4)
        image(1, a // 4, a // 4 + 4)
    lists(1, (1, 2, 3, 4))
    stow(0, "S")
    stow(1, "V")
    for P, q in ((2, "S"), (3, "V")):
        gather(P, q, 0, 32)
        image(P, 0, 8)
        stow(P, q)

    w = 128 // R
    for P in range(2):
        rs = range(P * R // 2, (P + 1) * R // 2)
        n = len(on) // len(rs)
        order_after("G", ["send%d" % P], [])
        write(g, topo, core, [(relays[r][0], T.hop2[:], T.sendAB[:, w * r:w * r + w], on[i * n:(i + 1) * n])
                              for i, r in enumerate(rs)], sem.r2, sem.loc)
        total["loc"] += len(on)
    for P, qs in zip((2, 3), mine):
        n = len(off) // len(qs)
        order_after("G", ["send%d" % P], [])
        at = [64 * (P - 2) + 32 * (order.index(q) % 2) for q in qs]
        write(g, topo, core, [(T.cores[q], T.land2[:, slot], T.sendCD[:, c:c + 32], off[i * n:(i + 1) * n])
                              for i, (q, c) in enumerate(zip(qs, at))], sem.a2d, sem.loc)
        total["loc"] += n * len(qs)
    total["a2d"] = sum(len(off) // len(qs) for q in same for qs in direct(T, topo, T.cores[q])[1] if rank in qs)
    total["a2x"] = len(cross) * (len(off) // (len(cross) // R))
    wrote["land2d"], wrote["land2x"] = ("a2d", total["a2d"]), ("a2x", total["a2x"])

    ts(["rown", "k32"], ["prm0"], T.prm[:], T.rown[0:32, 0:8], 32.0, fc(23, 32), A.mult, A.is_equal)
    tt(["cc", "k32"], ["wc"], T.wc[:], T.cc[:], fc(23, 32), A.add)
    ts(["prm0", "isA"], ["prm"], T.prm[:], T.prm[:], fc(9, 32), None, A.mult)
    mm("b5", T.b5[0:1, 0:8], [(T.wc[:], T.prm[:], ["wc", "prm"])])
    cp(["b5"], ["wrow"], T.wrow[:], T.b5[0:1, 0:8])
    dma("Y", "dw", T.w[:], T.wrow[:], ["wrow"], ["w"])

    i = order.index(rank)
    c = 64 * (i // 2 - 2) + 32 * (i % 2)
    sumup("b4", T.land2, T.sendCD[:, c:c + 32], ["send%d" % (i // 2)], "land2")
    cp(["b4"], ["yo"], T.yo[:], T.b4[:, 0:32])
    dma("Y", "dy", T.y[:], T.yo[:], ["yo"], ["y"])
    wait("Y", "dw", total["dw"])
    wait("Y", "dy", total["dy"])
    for name in sorted(total):
        if max(known[q].get(name, 0) for q in eng) < total[name]:
            wait("G", name, total[name])
